import numpy as np
import ml_dtypes


def mxq(x, axis, fmt="e4m3"):
    dtype, down = {"e4m3": (ml_dtypes.float8_e4m3fn, 7), "e5m2": (ml_dtypes.float8_e5m2, 14)}[fmt]
    v = np.moveaxis(np.asarray(x, np.float32).astype(ml_dtypes.bfloat16).astype(np.float64), axis, -1)
    blocks = v.reshape(v.shape[:-1] + (-1, 32))
    amax = np.abs(blocks).max(-1, keepdims=True)
    byte = np.maximum(np.where(amax > 0, np.frexp(amax)[1] - 1 + 127, 0) - down, 1)
    scale = np.exp2(byte - 127.0)
    codes = (blocks / scale).astype(np.float32).astype(dtype).astype(np.float64)
    return np.moveaxis((codes * scale).reshape(v.shape), -1, axis)


WIDE = False


def mx_kscale(k):
    if not WIDE:
        return np.ones(k)
    levels = np.array([10, -10, 5, -5, 0])
    if k % 512:
        return np.exp2(np.random.permutation(np.resize(levels, k // 32))).repeat(32)
    a = np.empty((k // 512, 16))
    for p in range(k // 512):
        a[p, :8] = np.random.permutation(np.resize(levels, 8))
        for g in range(8):
            far = levels[np.abs(levels - a[p, g]) >= 10]
            a[p, g + 8] = far[np.random.randint(len(far))]
    return np.exp2(a.ravel()).repeat(32)


def f64(x):
    return np.asarray(x).astype(np.float64)


def striped8(idx):
    return np.asarray(idx).reshape(8, -1, 16).transpose(0, 2, 1).reshape(128, -1).astype(np.uint16)


def unstriped8(offs):
    return offs.reshape(8, 16, -1).transpose(0, 2, 1).reshape(8, -1).astype(np.int64)


def pick8(x, idx, run):
    r = np.arange(len(x))
    return x[r[:, None], idx[r % (8 * run) // run]]


E2M1 = np.array([0.0, 0.5, 1.0, 1.5, 2.0, 3.0, 4.0, 6.0, -0.0, -0.5, -1.0, -1.5, -2.0, -3.0, -4.0, -6.0])


def pack_weight(w, fmt):
    k, n = w.shape
    w = f64(np.asarray(w, np.float32).astype(ml_dtypes.bfloat16)).reshape(k // 32, 32, n)
    amax = np.abs(w).max(1)
    if fmt == "e4m3":
        byte = np.frexp(amax)[1] - 1 + 127 - 7
    else:
        mant, ex = np.frexp(amax / 6.0)
        byte = np.where(mant > 0.5, ex, ex - 1) + 127
    byte = np.clip(np.where(amax > 0, byte, 1), 1, 254)
    scaled = (w * np.exp2(127.0 - byte)[:, None, :]).reshape(k, n).astype(np.float32)
    by_word = np.ascontiguousarray(scaled.reshape(k // 512, 128, 4, n).transpose(0, 1, 3, 2))
    if fmt == "e4m3":
        words = by_word.astype(ml_dtypes.float8_e4m3fn).view(np.uint8)
    else:
        c = by_word.astype(ml_dtypes.float4_e2m1fn).view(np.uint8) & 0xF
        words = (c[..., 0::2] | (c[..., 1::2] << 4)).reshape(k // 512, 128, 2 * n)
    return np.ascontiguousarray(words), np.ascontiguousarray(byte.astype(np.uint8).reshape(k // 512, 16, n))


def unpack_weight(words, scales, fmt):
    g, _, n = scales.shape
    words = np.ascontiguousarray(words).reshape(g, 128, n, -1)
    if fmt == "e4m3":
        vals = words.view(ml_dtypes.float8_e4m3fn).astype(np.float64)
    else:
        nib = np.empty((g, 128, n, 4), np.uint8)
        nib[..., 0::2] = words & 0xF
        nib[..., 1::2] = words >> 4
        vals = E2M1[nib]
    vals = vals * np.repeat(np.exp2(scales.astype(np.float64) - 127.0), 8, axis=1)[..., None]
    return vals.transpose(0, 1, 3, 2).reshape(g * 512, n)


D, T, I, Q = 512, 1024, 512, 128


def setup_inputs():
    n = np.random.standard_normal
    idx = np.stack([np.random.permutation(T)[:I] for _ in range(8)])
    idx2 = np.stack([np.random.permutation(T)[:I] for _ in range(8)])
    idx3 = np.stack([np.random.permutation(T)[:I] for _ in range(8)])
    fd = mx_kscale(D)
    keysp = pack_weight(n((D, T)) / fd[:, None], "e4m3")
    return {
        "query": (n((D, Q)) * 0.9 / np.sqrt(D) * fd[:, None]).astype(np.float32),
        "query2": (n((D, Q)) * 0.9 / np.sqrt(D) * fd[:, None]).astype(np.float32),
        "keys_words": keysp[0],
        "keys_scales": keysp[1],
        "lam": (np.random.uniform(0.5, 1.3, (Q, 1))).astype(np.float32),
        "old": (1.0 * n((Q, T))).astype(np.float32),
        "share2": (np.random.uniform(0.4, 1.2, (Q, 1))).astype(np.float32),
        "offs": striped8(idx),
        "offs2": striped8(idx2),
        "offs3": striped8(idx3),
    }


def reference(query, query2, keys_words, keys_scales, lam, old, share2, offs, offs2, offs3):
    idx = unstriped8(offs)
    idx2 = unstriped8(offs2)
    idx3 = unstriped8(offs3)
    keysu = unpack_weight(keys_words, keys_scales, "e4m3")
    queryq = mxq(f64(query), 0, "e4m3")
    a = queryq.T @ keysu
    query2q = mxq(f64(query2), 0, "e4m3")
    b = query2q.T @ keysu
    w = (np.maximum(pick8(a, idx, 16), pick8(b, idx2, 16)) - np.maximum(pick8(a, idx2, 16), pick8(b, idx, 16))) * f64(lam)
    f1 = np.zeros((Q, T))
    f1[np.arange(Q)[:, None], idx[np.arange(Q) % 128 // 16]] = w
    f2 = np.zeros((Q, T))
    f2[np.arange(Q)[:, None], idx3[np.arange(Q) % 128 // 16]] = w
    y = f64(old) + f1 + f2 * f64(share2)
    return y

@@ -1,0 +1,146 @@
+from contextlib import ExitStack
+
+import concourse.mybir as mybir
+
+D, T, I, Q = 512, 1024, 512, 128
+FLOPS = 2 * 2 * D * Q * T
+
+F32 = mybir.dt.float32
+BF16 = mybir.dt.bfloat16
+I32 = mybir.dt.int32
+U32 = mybir.dt.uint32
+U16 = mybir.dt.uint16
+U8 = mybir.dt.uint8
+FP8X4 = mybir.dt.float8_e4m3fn_x4
+ALU = mybir.AluOpType
+COPY = mybir.ActivationFunctionType.Copy
+
+P = 128
+PACK = 4
+HALF = I // 2
+LIST_COLS = I // 16
+
+
+def tile_attend_exchanged_lean_twiceput_heads_kernel(
+    tc, query, query2, keys_words, keys_scales, lam, old, share2, offs, offs2, offs3, out
+):
+    nc = tc.nc
+    with ExitStack() as ctx:
+        sb = ctx.enter_context(tc.tile_pool(name="sb", bufs=1))
+        ps = ctx.enter_context(tc.psum_pool(name="ps", bufs=1))
+
+        list1 = sb.tile([P, LIST_COLS], U16, name="list1")
+        list2 = sb.tile([P, LIST_COLS], U16, name="list2")
+        list3 = sb.tile([P, LIST_COLS], U16, name="list3")
+
+        key_scale = sb.tile([P, T], U8, name="key_scale", align_bytes=64)
+        for quad in range(4):
+            nc.scalar.dma_start(
+                out=key_scale[32 * quad : 32 * quad + 4, :].bitcast(I32),
+                in_=keys_scales[0, 4 * quad : 4 * quad + 4, :].bitcast(I32),
+            )
+
+        words = keys_words[0].rearrange("p n r -> p (n r)").bitcast(I32)
+        raw_a = sb.tile([P, PACK, Q], F32, name="raw_a")
+        raw_b = sb.tile([P, PACK, Q], F32, name="raw_b")
+        key_lo = sb.tile([P, T // 2], U32, name="key_lo", align_bytes=64)
+        key_hi = sb.tile([P, T // 2], U32, name="key_hi", align_bytes=64)
+        old_sb = sb.tile([P, T], F32, name="old_sb")
+        nc.sync.dma_start(out=raw_a[:], in_=query.rearrange("(p j) q -> p j q", j=PACK))
+        nc.sync.dma_start(out=key_lo[:].bitcast(I32), in_=words[:, : T // 2])
+        nc.sync.dma_start(out=raw_b[:], in_=query2.rearrange("(p j) q -> p j q", j=PACK))
+        nc.sync.dma_start(out=key_hi[:].bitcast(I32), in_=words[:, T // 2 :])
+        nc.sync.dma_start(list1[:], offs)
+        nc.sync.dma_start(list2[:], offs2)
+        nc.sync.dma_start(list3[:], offs3)
+        nc.sync.dma_start(out=old_sb[:], in_=old)
+
+        lam_sb = sb.tile([P, 1], F32, name="lam_sb")
+        share_sb = sb.tile([P, 1], F32, name="share_sb")
+        lam_share = sb.tile([P, 1], F32, name="lam_share")
+        nc.gpsimd.dma_start(out=lam_sb[:], in_=lam)
+        nc.gpsimd.dma_start(out=share_sb[:], in_=share2)
+        nc.gpsimd.tensor_tensor(lam_share[:], lam_sb[:], share_sb[:], ALU.mult)
+
+        put1 = sb.tile([P, T], F32, name="put1")
+        put3 = sb.tile([P, T], F32, name="put3")
+        nc.vector.memset(put1[:], 0.0)
+        nc.vector.memset(put3[:], 0.0)
+
+        def quantise(raw, name, on_scalar):
+            grouped = sb.tile([P, Q, PACK], BF16, name=name + "_grouped", align_bytes=64)
+            codes = sb.tile([P, Q], U32, name=name + "_codes", align_bytes=64)
+            scale = sb.tile([P, Q], U8, name=name + "_scale", align_bytes=64)
+            if on_scalar:
+                nc.scalar.activation(grouped[:], raw[:].rearrange("p j q -> p q j"), COPY)
+            else:
+                nc.vector.tensor_copy(out=grouped[:], in_=raw[:].rearrange("p j q -> p q j"))
+            nc.vector.quantize_mx(
+                out=codes[:].bitcast(FP8X4), scales=scale[:], in_=grouped[:].rearrange("p q j -> p (q j)")
+            )
+            return codes, scale
+
+        def score(codes, scale, dest, t0, width, engine_copy, name):
+            bank = ps.tile([P, width], F32, name=name)
+            keys = key_lo if t0 < T // 2 else key_hi
+            k0 = t0 % (T // 2)
+            nc.tensor.matmul_mx(
+                out=bank[:],
+                lhsT=codes[:].bitcast(FP8X4),
+                lhsT_scale=scale[:],
+                rhs=keys[:, k0 : k0 + width].bitcast(FP8X4),
+                rhs_scale=key_scale[:, t0 : t0 + width],
+                start=True,
+                stop=True,
+            )
+            engine_copy(dest[:, t0 : t0 + width], bank[:])
+
+        a_sb = sb.tile([P, T], F32, name="a_sb")
+        b_sb = sb.tile([P, T], F32, name="b_sb")
+        a_codes, a_scale = quantise(raw_a, "a", False)
+        b_codes, b_scale = quantise(raw_b, "b", True)
+        score(a_codes, a_scale, a_sb, 0, 512, nc.scalar.copy, "bank_a0")
+        score(a_codes, a_scale, a_sb, 512, 256, nc.scalar.copy, "bank_a1")
+        score(a_codes, a_scale, a_sb, 768, 256, nc.vector.tensor_copy, "bank_a2")
+        for n in range(4):
+            score(b_codes, b_scale, b_sb, 256 * n, 256, nc.scalar.copy, "bank_b%d" % n)
+
+        a_first = sb.tile([P, I], F32, name="a_first")
+        a_second = sb.tile([P, I], F32, name="a_second")
+        b_second = sb.tile([P, I], F32, name="b_second")
+        neg_b_first = sb.tile([P, I], F32, name="neg_b_first")
+        upper = sb.tile([P, I], F32, name="upper")
+        neg_lower = sb.tile([P, I], F32, name="neg_lower")
+
+        def slots(h):
+            return slice(h * HALF, (h + 1) * HALF)
+
+        def cols(h):
+            return slice(h * LIST_COLS // 2, (h + 1) * LIST_COLS // 2)
+
+        def larger(h):
+            s = slots(h)
+            nc.vector.scalar_tensor_tensor(neg_lower[:, s], a_second[:, s], -1.0, neg_b_first[:, s], ALU.mult, ALU.min)
+            nc.vector.tensor_tensor(upper[:, s], a_first[:, s], b_second[:, s], ALU.max)
+
+        nc.vector.tensor_copy(a_first[:, slots(0)], a_sb[:].indirect(list1[:, cols(0)]))
+        nc.vector.tensor_copy(a_second[:, slots(0)], a_sb[:].indirect(list2[:, cols(0)]))
+        nc.vector.tensor_copy(b_second[:, slots(0)], b_sb[:].indirect(list2[:, cols(0)]))
+        nc.scalar.activation(neg_b_first[:, slots(0)], b_sb[:].indirect(list1[:, cols(0)]), COPY, scale=-1.0)
+        larger(0)
+        nc.scalar.activation(a_second[:, slots(1)], a_sb[:].indirect(list2[:, cols(1)]), COPY)
+        nc.scalar.activation(neg_b_first[:, slots(1)], b_sb[:].indirect(list1[:, cols(1)]), COPY, scale=-1.0)
+        nc.scalar.activation(a_first[:, slots(1)], a_sb[:].indirect(list1[:, cols(1)]), COPY)
+        nc.scalar.activation(b_second[:, slots(1)], b_sb[:].indirect(list2[:, cols(1)]), COPY)
+        nc.vector.tensor_tensor(put1[:].indirect(list1[:, cols(0)]), upper[:, slots(0)], neg_lower[:, slots(0)], ALU.add)
+        larger(1)
+        nc.vector.tensor_tensor(put1[:].indirect(list1[:, cols(1)]), upper[:, slots(1)], neg_lower[:, slots(1)], ALU.add)
+        nc.vector.tensor_tensor(put3[:].indirect(list3[:]), upper[:], neg_lower[:], ALU.add)
+
+        partial = sb.tile([P, T], F32, name="partial")
+        result = sb.tile([P, T], F32, name="result")
+        nc.vector.scalar_tensor_tensor(partial[:], put1[:], lam_sb[:], old_sb[:], ALU.mult, ALU.add)
+        for n in range(4):
+            c = slice(256 * n, 256 * (n + 1))
+            nc.vector.scalar_tensor_tensor(result[:, c], put3[:, c], lam_share[:], partial[:, c], ALU.mult, ALU.add)
+            nc.sync.dma_start(out=out[:, c], in_=result[:, c])

@@ -1,6 +1,7 @@
 from contextlib import ExitStack
 
 import concourse.mybir as mybir
+from concourse.masks import make_identity
 
 D, T, I, Q = 512, 1024, 512, 128
 FLOPS = 2 * 2 * D * Q * T
@@ -34,11 +35,6 @@ def tile_attend_exchanged_lean_twiceput_heads_kernel(
         list3 = sb.tile([P, LIST_COLS], U16, name="list3")
 
         key_scale = sb.tile([P, T], U8, name="key_scale", align_bytes=64)
-        for quad in range(4):
-            nc.scalar.dma_start(
-                out=key_scale[32 * quad : 32 * quad + 4, :].bitcast(I32),
-                in_=keys_scales[0, 4 * quad : 4 * quad + 4, :].bitcast(I32),
-            )
 
         words = keys_words[0].rearrange("p n r -> p (n r)").bitcast(I32)
         raw_a = sb.tile([P, PACK, Q], F32, name="raw_a")
@@ -47,6 +43,11 @@ def tile_attend_exchanged_lean_twiceput_heads_kernel(
         key_hi = sb.tile([P, T // 2], U32, name="key_hi", align_bytes=64)
         old_sb = sb.tile([P, T], F32, name="old_sb")
         nc.sync.dma_start(out=raw_a[:], in_=query.rearrange("(p j) q -> p j q", j=PACK))
+        for quad in range(4):
+            nc.sync.dma_start(
+                out=key_scale[32 * quad : 32 * quad + 4, :].bitcast(I32),
+                in_=keys_scales[0, 4 * quad : 4 * quad + 4, :].bitcast(I32),
+            )
         nc.sync.dma_start(out=key_lo[:].bitcast(I32), in_=words[:, : T // 2])
         nc.sync.dma_start(out=raw_b[:], in_=query2.rearrange("(p j) q -> p j q", j=PACK))
         nc.sync.dma_start(out=key_hi[:].bitcast(I32), in_=words[:, T // 2 :])
@@ -58,8 +59,8 @@ def tile_attend_exchanged_lean_twiceput_heads_kernel(
         lam_sb = sb.tile([P, 1], F32, name="lam_sb")
         share_sb = sb.tile([P, 1], F32, name="share_sb")
         lam_share = sb.tile([P, 1], F32, name="lam_share")
-        nc.gpsimd.dma_start(out=lam_sb[:], in_=lam)
-        nc.gpsimd.dma_start(out=share_sb[:], in_=share2)
+        nc.sync.dma_start(out=lam_sb[:], in_=lam)
+        nc.sync.dma_start(out=share_sb[:], in_=share2)
         nc.gpsimd.tensor_tensor(lam_share[:], lam_sb[:], share_sb[:], ALU.mult)
 
         put1 = sb.tile([P, T], F32, name="put1")
@@ -81,11 +82,12 @@ def tile_attend_exchanged_lean_twiceput_heads_kernel(
             return codes, scale
 
         def score(codes, scale, dest, t0, width, engine_copy, name):
-            bank = ps.tile([P, width], F32, name=name)
+            whole = ps.tile([P, 512], F32, name=name)
+            bank = whole[:, :width]
             keys = key_lo if t0 < T // 2 else key_hi
             k0 = t0 % (T // 2)
             nc.tensor.matmul_mx(
-                out=bank[:],
+                out=bank,
                 lhsT=codes[:].bitcast(FP8X4),
                 lhsT_scale=scale[:],
                 rhs=keys[:, k0 : k0 + width].bitcast(FP8X4),
@@ -93,17 +95,20 @@ def tile_attend_exchanged_lean_twiceput_heads_kernel(
                 start=True,
                 stop=True,
             )
-            engine_copy(dest[:, t0 : t0 + width], bank[:])
+            engine_copy(dest[:, t0 : t0 + width], bank)
 
         a_sb = sb.tile([P, T], F32, name="a_sb")
         b_sb = sb.tile([P, T], F32, name="b_sb")
         a_codes, a_scale = quantise(raw_a, "a", False)
-        b_codes, b_scale = quantise(raw_b, "b", True)
-        score(a_codes, a_scale, a_sb, 0, 512, nc.scalar.copy, "bank_a0")
-        score(a_codes, a_scale, a_sb, 512, 256, nc.scalar.copy, "bank_a1")
-        score(a_codes, a_scale, a_sb, 768, 256, nc.vector.tensor_copy, "bank_a2")
+        b_codes, b_scale = quantise(raw_b, "b", False)
+
+        def scalar_copy(dest, src):
+            nc.scalar.activation(dest, src, COPY)
+
         for n in range(4):
-            score(b_codes, b_scale, b_sb, 256 * n, 256, nc.scalar.copy, "bank_b%d" % n)
+            score(a_codes, a_scale, a_sb, 256 * n, 256, scalar_copy if n < 3 else nc.vector.tensor_copy, "bank_a%d" % n)
+        for n in range(4):
+            score(b_codes, b_scale, b_sb, 256 * n, 256, scalar_copy, "bank_b%d" % n)
 
         a_first = sb.tile([P, I], F32, name="a_first")
         a_second = sb.tile([P, I], F32, name="a_second")
@@ -137,10 +142,34 @@ def tile_attend_exchanged_lean_twiceput_heads_kernel(
         nc.vector.tensor_tensor(put1[:].indirect(list1[:, cols(1)]), upper[:, slots(1)], neg_lower[:, slots(1)], ALU.add)
         nc.vector.tensor_tensor(put3[:].indirect(list3[:]), upper[:], neg_lower[:], ALU.add)
 
-        partial = sb.tile([P, T], F32, name="partial")
+        ident = sb.tile([P, P], F32, name="ident")
+        make_identity(nc, ident[:])
+        scaled = sb.tile([P, T], F32, name="scaled")
+        turned = sb.tile([P, T], F32, name="turned")
         result = sb.tile([P, T], F32, name="result")
-        nc.vector.scalar_tensor_tensor(partial[:], put1[:], lam_sb[:], old_sb[:], ALU.mult, ALU.add)
+        turn_banks = [ps.tile([P, 512], F32, name=nm) for nm in ("bank_a0", "bank_a1", "bank_a2", "bank_a3")]
+        back_banks = [ps.tile([P, 512], F32, name="bank_b%d" % n) for n in range(4)]
+
+        def turn(dest, src, start, stop):
+            nc.tensor.matmul(dest, src, ident[:], start=start, stop=stop, is_transpose=True)
+
+        for n in range(4):
+            for j in range(2):
+                c = slice(256 * n + P * j, 256 * n + P * (j + 1))
+                turn(turn_banks[n][:, P * j : P * (j + 1)], old_sb[:, c], j == 0, False)
         for n in range(4):
             c = slice(256 * n, 256 * (n + 1))
-            nc.vector.scalar_tensor_tensor(result[:, c], put3[:, c], lam_share[:], partial[:, c], ALU.mult, ALU.add)
+            nc.scalar.activation(scaled[:, c], put1[:, c], COPY, scale=lam_sb[:])
+            for j in range(2):
+                c = slice(256 * n + P * j, 256 * n + P * (j + 1))
+                turn(turn_banks[n][:, P * j : P * (j + 1)], scaled[:, c], False, j == 1)
+        for n in range(4):
+            c = slice(256 * n, 256 * (n + 1))
+            nc.scalar.copy(turned[:, c], turn_banks[n][:, :256])
+            for j in range(2):
+                c = slice(256 * n + P * j, 256 * n + P * (j + 1))
+                turn(back_banks[n][:, P * j : P * (j + 1)], turned[:, c], True, True)
+        for n in range(4):
+            c = slice(256 * n, 256 * (n + 1))
+            nc.vector.scalar_tensor_tensor(result[:, c], put3[:, c], lam_share[:], back_banks[n][:, :256], ALU.mult, ALU.add)
             nc.sync.dma_start(out=out[:, c], in_=result[:, c])

from contextlib import ExitStack

import concourse.mybir as mybir
from concourse.masks import make_identity

D, T, I, Q = 512, 1024, 512, 128
FLOPS = 2 * 2 * D * Q * T

F32 = mybir.dt.float32
BF16 = mybir.dt.bfloat16
I32 = mybir.dt.int32
U32 = mybir.dt.uint32
U16 = mybir.dt.uint16
U8 = mybir.dt.uint8
FP8X4 = mybir.dt.float8_e4m3fn_x4
ALU = mybir.AluOpType
COPY = mybir.ActivationFunctionType.Copy

P = 128
PACK = 4
HALF = I // 2
LIST_COLS = I // 16


def tile_attend_exchanged_lean_twiceput_heads_kernel(
    tc, query, query2, keys_words, keys_scales, lam, old, share2, offs, offs2, offs3, out
):
    nc = tc.nc
    with ExitStack() as ctx:
        sb = ctx.enter_context(tc.tile_pool(name="sb", bufs=1))
        ps = ctx.enter_context(tc.psum_pool(name="ps", bufs=1))

        list1 = sb.tile([P, LIST_COLS], U16, name="list1")
        list2 = sb.tile([P, LIST_COLS], U16, name="list2")
        list3 = sb.tile([P, LIST_COLS], U16, name="list3")

        key_scale = sb.tile([P, T], U8, name="key_scale", align_bytes=64)

        words = keys_words[0].rearrange("p n r -> p (n r)").bitcast(I32)
        raw_a = sb.tile([P, PACK, Q], F32, name="raw_a")
        raw_b = sb.tile([P, PACK, Q], F32, name="raw_b")
        key_lo = sb.tile([P, T // 2], U32, name="key_lo", align_bytes=64)
        key_hi = sb.tile([P, T // 2], U32, name="key_hi", align_bytes=64)
        old_sb = sb.tile([P, T], F32, name="old_sb")
        nc.sync.dma_start(out=raw_a[:], in_=query.rearrange("(p j) q -> p j q", j=PACK))
        for quad in range(4):
            nc.sync.dma_start(
                out=key_scale[32 * quad : 32 * quad + 4, :].bitcast(I32),
                in_=keys_scales[0, 4 * quad : 4 * quad + 4, :].bitcast(I32),
            )
        nc.sync.dma_start(out=key_lo[:].bitcast(I32), in_=words[:, : T // 2])
        nc.sync.dma_start(out=raw_b[:], in_=query2.rearrange("(p j) q -> p j q", j=PACK))
        nc.sync.dma_start(out=key_hi[:].bitcast(I32), in_=words[:, T // 2 :])
        nc.sync.dma_start(list1[:], offs)
        nc.sync.dma_start(list2[:], offs2)
        nc.sync.dma_start(list3[:], offs3)
        nc.sync.dma_start(out=old_sb[:], in_=old)

        lam_sb = sb.tile([P, 1], F32, name="lam_sb")
        share_sb = sb.tile([P, 1], F32, name="share_sb")
        lam_share = sb.tile([P, 1], F32, name="lam_share")
        nc.sync.dma_start(out=lam_sb[:], in_=lam)
        nc.sync.dma_start(out=share_sb[:], in_=share2)
        nc.gpsimd.tensor_tensor(lam_share[:], lam_sb[:], share_sb[:], ALU.mult)

        put1 = sb.tile([P, T], F32, name="put1")
        put3 = sb.tile([P, T], F32, name="put3")
        nc.vector.memset(put1[:], 0.0)
        nc.vector.memset(put3[:], 0.0)

        def quantise(raw, name, on_scalar):
            grouped = sb.tile([P, Q, PACK], BF16, name=name + "_grouped", align_bytes=64)
            codes = sb.tile([P, Q], U32, name=name + "_codes", align_bytes=64)
            scale = sb.tile([P, Q], U8, name=name + "_scale", align_bytes=64)
            if on_scalar:
                nc.scalar.activation(grouped[:], raw[:].rearrange("p j q -> p q j"), COPY)
            else:
                nc.vector.tensor_copy(out=grouped[:], in_=raw[:].rearrange("p j q -> p q j"))
            nc.vector.quantize_mx(
                out=codes[:].bitcast(FP8X4), scales=scale[:], in_=grouped[:].rearrange("p q j -> p (q j)")
            )
            return codes, scale

        def score(codes, scale, dest, t0, width, engine_copy, name):
            whole = ps.tile([P, 512], F32, name=name)
            bank = whole[:, :width]
            keys = key_lo if t0 < T // 2 else key_hi
            k0 = t0 % (T // 2)
            nc.tensor.matmul_mx(
                out=bank,
                lhsT=codes[:].bitcast(FP8X4),
                lhsT_scale=scale[:],
                rhs=keys[:, k0 : k0 + width].bitcast(FP8X4),
                rhs_scale=key_scale[:, t0 : t0 + width],
                start=True,
                stop=True,
            )
            engine_copy(dest[:, t0 : t0 + width], bank)

        a_sb = sb.tile([P, T], F32, name="a_sb")
        b_sb = sb.tile([P, T], F32, name="b_sb")
        a_codes, a_scale = quantise(raw_a, "a", False)
        b_codes, b_scale = quantise(raw_b, "b", False)

        def scalar_copy(dest, src):
            nc.scalar.activation(dest, src, COPY)

        for n in range(4):
            score(a_codes, a_scale, a_sb, 256 * n, 256, scalar_copy if n < 3 else nc.vector.tensor_copy, "bank_a%d" % n)
        for n in range(4):
            score(b_codes, b_scale, b_sb, 256 * n, 256, scalar_copy, "bank_b%d" % n)

        a_first = sb.tile([P, I], F32, name="a_first")
        a_second = sb.tile([P, I], F32, name="a_second")
        b_second = sb.tile([P, I], F32, name="b_second")
        neg_b_first = sb.tile([P, I], F32, name="neg_b_first")
        upper = sb.tile([P, I], F32, name="upper")
        neg_lower = sb.tile([P, I], F32, name="neg_lower")

        def slots(h):
            return slice(h * HALF, (h + 1) * HALF)

        def cols(h):
            return slice(h * LIST_COLS // 2, (h + 1) * LIST_COLS // 2)

        def larger(h):
            s = slots(h)
            nc.vector.scalar_tensor_tensor(neg_lower[:, s], a_second[:, s], -1.0, neg_b_first[:, s], ALU.mult, ALU.min)
            nc.vector.tensor_tensor(upper[:, s], a_first[:, s], b_second[:, s], ALU.max)

        nc.vector.tensor_copy(a_first[:, slots(0)], a_sb[:].indirect(list1[:, cols(0)]))
        nc.vector.tensor_copy(a_second[:, slots(0)], a_sb[:].indirect(list2[:, cols(0)]))
        nc.vector.tensor_copy(b_second[:, slots(0)], b_sb[:].indirect(list2[:, cols(0)]))
        nc.scalar.activation(neg_b_first[:, slots(0)], b_sb[:].indirect(list1[:, cols(0)]), COPY, scale=-1.0)
        larger(0)
        nc.scalar.activation(a_second[:, slots(1)], a_sb[:].indirect(list2[:, cols(1)]), COPY)
        nc.scalar.activation(neg_b_first[:, slots(1)], b_sb[:].indirect(list1[:, cols(1)]), COPY, scale=-1.0)
        nc.scalar.activation(a_first[:, slots(1)], a_sb[:].indirect(list1[:, cols(1)]), COPY)
        nc.scalar.activation(b_second[:, slots(1)], b_sb[:].indirect(list2[:, cols(1)]), COPY)
        nc.vector.tensor_tensor(put1[:].indirect(list1[:, cols(0)]), upper[:, slots(0)], neg_lower[:, slots(0)], ALU.add)
        larger(1)
        nc.vector.tensor_tensor(put1[:].indirect(list1[:, cols(1)]), upper[:, slots(1)], neg_lower[:, slots(1)], ALU.add)
        nc.vector.tensor_tensor(put3[:].indirect(list3[:]), upper[:], neg_lower[:], ALU.add)

        ident = sb.tile([P, P], F32, name="ident")
        make_identity(nc, ident[:])
        scaled = sb.tile([P, T], F32, name="scaled")
        turned = sb.tile([P, T], F32, name="turned")
        result = sb.tile([P, T], F32, name="result")
        turn_banks = [ps.tile([P, 512], F32, name=nm) for nm in ("bank_a0", "bank_a1", "bank_a2", "bank_a3")]
        back_banks = [ps.tile([P, 512], F32, name="bank_b%d" % n) for n in range(4)]

        def turn(dest, src, start, stop):
            nc.tensor.matmul(dest, src, ident[:], start=start, stop=stop, is_transpose=True)

        for n in range(4):
            for j in range(2):
                c = slice(256 * n + P * j, 256 * n + P * (j + 1))
                turn(turn_banks[n][:, P * j : P * (j + 1)], old_sb[:, c], j == 0, False)
        for n in range(4):
            c = slice(256 * n, 256 * (n + 1))
            nc.scalar.activation(scaled[:, c], put1[:, c], COPY, scale=lam_sb[:])
            for j in range(2):
                c = slice(256 * n + P * j, 256 * n + P * (j + 1))
                turn(turn_banks[n][:, P * j : P * (j + 1)], scaled[:, c], False, j == 1)
        for n in range(4):
            c = slice(256 * n, 256 * (n + 1))
            nc.scalar.copy(turned[:, c], turn_banks[n][:, :256])
            for j in range(2):
                c = slice(256 * n + P * j, 256 * n + P * (j + 1))
                turn(back_banks[n][:, P * j : P * (j + 1)], turned[:, c], True, True)
        for n in range(4):
            c = slice(256 * n, 256 * (n + 1))
            nc.vector.scalar_tensor_tensor(result[:, c], put3[:, c], lam_share[:], back_banks[n][:, :256], ALU.mult, ALU.add)
            nc.sync.dma_start(out=out[:, c], in_=result[:, c])
